import numpy as np, ml_dtypes
CORES = [13,21,141,149]
N = 4
DEG, TK = 3, 64
MASK = [[0,2,3],[1,2,3],[0,2,3],[0,2,3]]
def setup_inputs(rng):
    return {"x": rng.standard_normal((N, 128, TK), dtype=np.float32).astype(ml_dtypes.bfloat16), "w": rng.standard_normal((N, 128, DEG * 128), dtype=np.float32).astype(ml_dtypes.bfloat16)}
def setup_inputs_big(rng):
    d = setup_inputs(rng)
    for k in ("x", "w"): d[k] = (d[k].astype(np.float32) * 1024.0).astype(d[k].dtype)
    return d
def setup_inputs_small(rng):
    d = setup_inputs(rng)
    for k in ("x", "w"): d[k] = (d[k].astype(np.float32) * (1 / 1024.0)).astype(d[k].dtype)
    return d
def setup_inputs_apart(rng):
    d = setup_inputs(rng)
    f = (10.0 ** rng.permutation(np.linspace(-1.5, 1.5, N))).astype(np.float32).reshape(N, 1, 1)
    for k in ("x", "w"): d[k] = (d[k].astype(np.float32) * f).astype(d[k].dtype)
    return d
def reference(x, w):
    X, W = x.astype(np.float64), w.astype(np.float64)
    y = np.zeros((N, 128, TK))
    for r in range(N):
        for i, j in enumerate(MASK[r]):
            y[r] += W[r][:, 128 * i:128 * i + 128].T @ X[j]
    return {"y": y.astype(ml_dtypes.bfloat16 if x.dtype != np.float64 else np.float64)}

from concourse.bass import DstId, RemoteDMATransfer

P, TK = 128, 64
DEG = 3
K_HOP = 4
K_OUT = 8

SCRATCH = {
    "xd": ("dram", [P, TK], "bfloat16"),
    "xin": ("sbuf", [P, DEG * TK], "bfloat16"),
    "ws": ("sbuf", [P, DEG * P], "bfloat16"),
    "acc": ("psum", [P, TK], "float32"),
    "ys": ("sbuf", [P, TK], "bfloat16"),
}
SEMAPHORES = ["ld", "lw", "hop", "arr0", "arr1", "arr2", "sent", "mm", "cp", "st"]


def _engines(mask, n, avoid=0):
    bits = [b for b in range(mask.bit_length()) if (mask >> b) & 1]
    free = [b for b in bits if not (avoid >> b) & 1]
    if len(free) < n:
        free = bits
    out = 0
    for b in free[:n]:
        out |= 1 << b
    return out


def _plan(T, topo):
    cores, table = T.cores, T.tables["MASK"]
    world = range((max(topo.host(c) for c in cores) + 1) * topo.CORES_PER_HOST)
    direct, relay = {}, {}
    for j, src in enumerate(cores):
        direct[j], relay[j] = [], []
        near = [c for c in world if T.rank_of(c) is None and topo.host(c) == topo.host(src)
                and topo.chip(c) == topo.chip(src) and topo.die(c) == topo.die(src)]
        for r, dst in enumerate(cores):
            if r == j or j not in table[r]:
                continue
            slot = table[r].index(j)
            if topo.may_write(src, dst):
                direct[j].append((dst, slot))
            else:
                ports = [c for c in near if topo.may_write(c, dst)]
                relay[j].append((ports[len(relay[j]) % len(ports)], dst, slot))
    return direct, relay


def _slot(T, i):
    return T.xin[:, i * TK:(i + 1) * TK]


def _write(g, T, topo, core, dst, slot):
    rid, pid = topo.addr(dst, core)
    g.remote_dma(out_ap=_slot(T, slot), in_ap=T.xd[:], remote_sem=T.sem["arr%d" % slot], local_sem=T.sem.sent,
                 pid=pid, routing_id=rid, dma_engine_mask=_engines(topo.mask(core, dst), K_OUT))
    return K_OUT


def rank_program(g, core, T, topo):
    direct, relay = _plan(T, topo)
    sem = T.sem
    rank = T.rank_of(core)

    if rank is None:
        jobs = [(dst, slot) for j in relay for (h, dst, slot) in relay[j] if h == core]
        if not jobs:
            return
        g.wait_ge(sem.hop, K_HOP)
        n = 0
        for dst, slot in jobs:
            n += _write(g, T, topo, core, dst, slot)
        g.wait_ge(sem.sent, n)
        return

    tiles = T.tables["MASK"][rank]
    sends = bool(direct[rank] or relay[rank])

    if sends:
        g.sync.dma_start(T.xd[:], T.x[:]).then_inc(sem.ld, 16)
    n_lw = 16
    if rank in tiles:
        g.sync.dma_start(_slot(T, tiles.index(rank)), T.x[:]).then_inc(sem.lw, 16)
        n_lw += 16
    g.sync.dma_start(T.ws[:], T.w[:]).then_inc(sem.lw, 16)

    if sends:
        g.wait_ge(sem.ld, 16)
        n = 0
        off = 0
        for dst, _ in direct[rank]:
            off |= topo.mask(core, dst)
        helpers = []
        for h, _, _ in relay[rank]:
            if h not in helpers:
                helpers.append(h)
        if helpers:
            ids = []
            for h in helpers:
                rid, pid = topo.addr(h, core)
                ids.append(DstId(rid=rid, pnc=pid))
            g.remote_dma_fused([RemoteDMATransfer(
                dst_ids=ids, dma_engine_mask=_engines(topo.mask(core, helpers[0]), K_HOP, avoid=off),
                remote_sem=sem.hop, srcs=[T.xd[:]], dsts=[T.xd[:] for _ in helpers], alu_op=0)], local_sem=sem.sent)
            n += K_HOP
        for dst, slot in direct[rank]:
            n += _write(g, T, topo, core, dst, slot)

    def hops(i):
        j = tiles[i]
        return 0 if j == rank else (1 if topo.may_write(T.cores[j], core) else 2)
    order = sorted(range(len(tiles)), key=hops)
    g.tensor.wait_ge(sem.lw, n_lw)
    for k, i in enumerate(order):
        if tiles[i] != rank:
            g.tensor.wait_ge(sem["arr%d" % i], K_OUT)
        mm = g.tensor.matmul(T.acc[:], T.ws[:, i * P:(i + 1) * P], _slot(T, i), k == 0, k == len(order) - 1)
    mm.then_inc(sem.mm, 1)

    g.vector.wait_ge(sem.mm, 1)
    g.vector.tensor_copy(T.ys[:], T.acc[:]).then_inc(sem.cp, 1)
    g.sync.wait_ge(sem.cp, 1)
    g.sync.dma_start(T.y[:], T.ys[:]).then_inc(sem.st, 16)
    g.sync.wait_ge(sem.st, 16)
    if sends:
        g.wait_ge(sem.sent, n)
